import numpy as np
import ml_dtypes


def mxq(x, axis, fmt="e4m3"):
    dtype, down = {"e4m3": (ml_dtypes.float8_e4m3fn, 7), "e5m2": (ml_dtypes.float8_e5m2, 14)}[fmt]
    v = np.moveaxis(np.asarray(x, np.float32).astype(ml_dtypes.bfloat16).astype(np.float64), axis, -1)
    blocks = v.reshape(v.shape[:-1] + (-1, 32))
    amax = np.abs(blocks).max(-1, keepdims=True)
    byte = np.maximum(np.where(amax > 0, np.frexp(amax)[1] - 1 + 127, 0) - down, 1)
    scale = np.exp2(byte - 127.0)
    codes = (blocks / scale).astype(np.float32).astype(dtype).astype(np.float64)
    return np.moveaxis((codes * scale).reshape(v.shape), -1, axis)


WIDE = False


def mx_kscale(k):
    if not WIDE:
        return np.ones(k)
    levels = np.array([10, -10, 5, -5, 0])
    if k % 512:
        return np.exp2(np.random.permutation(np.resize(levels, k // 32))).repeat(32)
    a = np.empty((k // 512, 16))
    for p in range(k // 512):
        a[p, :8] = np.random.permutation(np.resize(levels, 8))
        for g in range(8):
            far = levels[np.abs(levels - a[p, g]) >= 10]
            a[p, g + 8] = far[np.random.randint(len(far))]
    return np.exp2(a.ravel()).repeat(32)


def f64(x):
    return np.asarray(x).astype(np.float64)


E2M1 = np.array([0.0, 0.5, 1.0, 1.5, 2.0, 3.0, 4.0, 6.0, -0.0, -0.5, -1.0, -1.5, -2.0, -3.0, -4.0, -6.0])


def pack_weight(w, fmt):
    k, n = w.shape
    w = f64(np.asarray(w, np.float32).astype(ml_dtypes.bfloat16)).reshape(k // 32, 32, n)
    amax = np.abs(w).max(1)
    if fmt == "e4m3":
        byte = np.frexp(amax)[1] - 1 + 127 - 7
    else:
        mant, ex = np.frexp(amax / 6.0)
        byte = np.where(mant > 0.5, ex, ex - 1) + 127
    byte = np.clip(np.where(amax > 0, byte, 1), 1, 254)
    scaled = (w * np.exp2(127.0 - byte)[:, None, :]).reshape(k, n).astype(np.float32)
    by_word = np.ascontiguousarray(scaled.reshape(k // 512, 128, 4, n).transpose(0, 1, 3, 2))
    if fmt == "e4m3":
        words = by_word.astype(ml_dtypes.float8_e4m3fn).view(np.uint8)
    else:
        c = by_word.astype(ml_dtypes.float4_e2m1fn).view(np.uint8) & 0xF
        words = (c[..., 0::2] | (c[..., 1::2] << 4)).reshape(k // 512, 128, 2 * n)
    return np.ascontiguousarray(words), np.ascontiguousarray(byte.astype(np.uint8).reshape(k // 512, 16, n))


def unpack_weight(words, scales, fmt):
    g, _, n = scales.shape
    words = np.ascontiguousarray(words).reshape(g, 128, n, -1)
    if fmt == "e4m3":
        vals = words.view(ml_dtypes.float8_e4m3fn).astype(np.float64)
    else:
        nib = np.empty((g, 128, n, 4), np.uint8)
        nib[..., 0::2] = words & 0xF
        nib[..., 1::2] = words >> 4
        vals = E2M1[nib]
    vals = vals * np.repeat(np.exp2(scales.astype(np.float64) - 127.0), 8, axis=1)[..., None]
    return vals.transpose(0, 1, 3, 2).reshape(g * 512, n)


K, M, T = 1536, 1536, 1024


def setup_inputs():
    n = np.random.standard_normal
    s = mx_kscale(K)[:, None]
    p_w4 = pack_weight(n((K, M)) / np.sqrt(K) / s ** 2, "e2m1")
    p_w8 = pack_weight(n((K, M)) / np.sqrt(K) / s, "e4m3")
    return {
        "x": (n((K, T)) * s).astype(np.float32),
        "w4_words": p_w4[0],
        "w4_scales": p_w4[1],
        "w8_words": p_w8[0],
        "w8_scales": p_w8[1],
    }


def reference(x, w4_words, w4_scales, w8_words, w8_scales):
    xa_, xb_ = mxq(f64(x) ** 2, 0, "e4m3"), mxq(f64(x), 0, "e4m3")
    w4_ = unpack_weight(w4_words, w4_scales, "e2m1")
    w8_ = unpack_weight(w8_words, w8_scales, "e4m3")
    y = xa_.T @ w4_ + xb_.T @ w8_
    return y

@@ -1,0 +1,206 @@
+from contextlib import ExitStack
+
+import concourse.mybir as mybir
+
+K, M, T = 1536, 1536, 1024
+FLOPS = 2 * 2 * K * M * T
+
+F32 = mybir.dt.float32
+BF16 = mybir.dt.bfloat16
+I32 = mybir.dt.int32
+U32 = mybir.dt.uint32
+U8 = mybir.dt.uint8
+FP8X4 = mybir.dt.float8_e4m3fn_x4
+FP4X4 = mybir.dt.float4_e2m1fn_x4
+SQUARE = mybir.ActivationFunctionType.Square
+
+P = 128
+PACK = 4
+K_PASS = P * PACK
+PASSES = K // K_PASS
+T_TILE = 128
+N_TILE = 512
+W8_ROW = 4
+
+
+def tile_mix_feat_tm_quad_none_kernel(tc, x, w4_words, w4_scales, w8_words, w8_scales, out):
+    nc = tc.nc
+
+    with ExitStack() as ctx:
+        keep = ctx.enter_context(tc.tile_pool(name="keep", bufs=1))
+        stage = ctx.enter_context(tc.tile_pool(name="stage", bufs=4))
+        results = ctx.enter_context(tc.tile_pool(name="results", bufs=16))
+        psum = ctx.enter_context(tc.psum_pool(name="psum", bufs=8))
+        ctx.enter_context(tc.manual_schedule())
+
+        w8_bytes = w8_words.rearrange("a p n i -> p a (n i)")
+        w4_bytes = w4_words.rearrange("a p b -> p a b")
+
+        raw = {}
+        w8 = {}
+        w4 = {}
+        feats = {}
+
+        def load_x(a, t0, nt):
+            tile = keep.tile([P, PACK, nt * T_TILE], F32, name="x_%d_%d" % (a, t0))
+            rows = x[a * K_PASS : (a + 1) * K_PASS, t0 * T_TILE : (t0 + nt) * T_TILE]
+            nc.sync.dma_start(out=tile[:], in_=rows.rearrange("(p j) w -> p j w", j=PACK))
+            for t in range(t0, t0 + nt):
+                raw[a, t] = (tile, (t - t0) * T_TILE)
+
+        def load_w8(a0, na, n0, nn):
+            tile = keep.tile([P, na, nn * N_TILE], U32, name="w8_%d_%d" % (a0, n0), align_bytes=256)
+            src = w8_bytes[:, a0 : a0 + na, 4 * n0 * N_TILE : 4 * (n0 + nn) * N_TILE]
+            nc.sync.dma_start(out=tile[:].bitcast(I32), in_=src.bitcast(I32))
+            for a in range(a0, a0 + na):
+                for n in range(n0, n0 + nn):
+                    w8[a, n] = tile[:, a - a0, (n - n0) * N_TILE : (n - n0 + 1) * N_TILE]
+
+        def load_w4(a0, na, n0, nn):
+            tile = keep.tile([P, na, 2 * nn * N_TILE], U8, name="w4_%d_%d" % (a0, n0), align_bytes=256)
+            src = w4_bytes[:, a0 : a0 + na, 2 * n0 * N_TILE : 2 * (n0 + nn) * N_TILE]
+            nc.sync.dma_start(out=tile[:].bitcast(I32), in_=src.bitcast(I32))
+            for a in range(a0, a0 + na):
+                for n in range(n0, n0 + nn):
+                    w4[a, n] = tile[:, a - a0, 2 * (n - n0) * N_TILE : 2 * (n - n0 + 1) * N_TILE]
+
+        def load_scales(plane, scales, row0):
+            by_row = scales.rearrange("a (q r) n -> r q a n", r=4)
+            for r in range(4):
+                nc.sync.dma_start(out=plane[row0 + r : P : 32, :, :].bitcast(I32), in_=by_row[r].bitcast(I32))
+
+        def widen(a, t0, nt):
+            tile, c0 = raw[a, t0]
+            width = nt * T_TILE
+            src = tile[:, :, c0 : c0 + width].rearrange("p j (c i) -> p c j i", i=4)
+            lin = stage.tile([P, width * PACK], BF16, name="lin", align_bytes=256)
+            sq = stage.tile([P, width * PACK], BF16, name="sq", align_bytes=256)
+            nc.vector.tensor_copy(out=lin[:].rearrange("p (c i j) -> p c j i", i=4, j=PACK), in_=src)
+            nc.scalar.activation(out=sq[:].rearrange("p (c i j) -> p c j i", i=4, j=PACK), in_=src, func=SQUARE)
+            return (a, t0, nt, lin, sq)
+
+        def quantize(unit):
+            a, t0, nt, lin, sq = unit
+            width = nt * T_TILE
+            for kind, src in (("lin", lin), ("sq", sq)):
+                codes = keep.tile([P, width], U32, name="%s_codes_%d_%d" % (kind, a, t0), align_bytes=256)
+                plane = keep.tile([P, width], U8, name="%s_plane_%d_%d" % (kind, a, t0), align_bytes=256)
+                nc.vector.quantize_mx(out=codes[:].bitcast(FP8X4), scales=plane[:], in_=src[:])
+                for t in range(t0, t0 + nt):
+                    cols = slice((t - t0) * T_TILE, (t - t0 + 1) * T_TILE)
+                    feats[kind, a, t] = (codes[:, cols], plane[:, cols])
+
+        def mm8(acc, a, t, n, c0, width, start):
+            codes, plane = feats["lin", a, t]
+            nc.tensor.matmul_mx(
+                out=acc[:, 0:width],
+                lhsT=codes.bitcast(FP8X4),
+                lhsT_scale=plane,
+                rhs=w8[a, n][:, c0 : c0 + width].bitcast(FP8X4),
+                rhs_scale=plane8[W8_ROW:P, a, n * N_TILE + c0 : n * N_TILE + c0 + width],
+                start=start,
+                stop=False,
+            )
+
+        def mm4(acc, a, t, n, c0, width, stop):
+            codes, plane = feats["sq", a, t]
+            step = N_TILE if width == N_TILE else 128
+            for s in range(0, width, step):
+                nc.tensor.matmul_mx(
+                    out=acc[:, s : s + step],
+                    lhsT=codes.bitcast(FP8X4),
+                    lhsT_scale=plane,
+                    rhs=w4[a, n][:, 2 * (c0 + s) : 2 * (c0 + s + step)].bitcast(FP4X4),
+                    rhs_scale=plane4[:, a, n * N_TILE + c0 + s : n * N_TILE + c0 + s + step],
+                    start=False,
+                    stop=stop and s + step == width,
+                )
+
+        drained = []
+
+        def drain(acc, t, n, c0, width):
+            res = results.tile([P, width], F32, name="res")
+            if len(drained) % 2 == 0:
+                nc.scalar.copy(out=res[:], in_=acc[:, 0:width])
+            else:
+                nc.vector.tensor_copy(out=res[:], in_=acc[:, 0:width])
+            drained.append((t, n, c0))
+            col = n * N_TILE + c0
+            nc.sync.dma_start(out=out[t * T_TILE : (t + 1) * T_TILE, col : col + width], in_=res[:])
+
+        def group(t, n, c0, width):
+            acc = psum.tile([P, N_TILE], F32, name="acc")
+            for a in range(PASSES):
+                mm8(acc, a, t, n, c0, width, a == 0)
+                mm4(acc, a, t, n, c0, width, a == PASSES - 1)
+            drain(acc, t, n, c0, width)
+
+        plane8 = keep.tile([P, PASSES, M], U8, name="plane8", align_bytes=256)
+        plane4 = keep.tile([P, PASSES, M], U8, name="plane4", align_bytes=256)
+        nc.vector.memset(plane8[:].bitcast(I32), 0)
+        nc.vector.memset(plane4[:].bitcast(I32), 0)
+
+        load_x(0, 0, 1)
+        load_w8(0, 1, 0, 1)
+        load_scales(plane8, w8_scales, W8_ROW)
+        load_x(0, 1, 1)
+        load_w8(0, 1, 1, 1)
+        load_w4(0, 1, 0, 2)
+        load_x(0, 2, 2)
+        load_scales(plane4, w4_scales, 0)
+        for a in range(1, PASSES):
+            load_x(a, 0, 2)
+            load_w8(a, 1, 0, 2)
+            load_w4(a, 1, 0, 2)
+            load_x(a, 2, 2)
+        load_w8(0, PASSES, 2, 1)
+        load_w4(0, PASSES, 2, 1)
+        for t0 in (4, 6):
+            for a in range(PASSES):
+                load_x(a, t0, 2)
+
+        accs = {}
+        for t in range(4):
+            for n in range(2):
+                acc = psum.tile([P, N_TILE], F32, name="acc")
+                accs[t, n] = acc
+        for a in range(PASSES):
+            for t0 in (0, 2):
+                if a == 0 and t0 == 0:
+                    quantize(widen(a, 0, 1))
+                    quantize(widen(a, 1, 1))
+                else:
+                    first = widen(a, t0, 1)
+                    second = widen(a, t0 + 1, 1)
+                    quantize(first)
+                    quantize(second)
+            for t0 in (0, 2):
+                if a < PASSES - 1:
+                    for n in range(2):
+                        for t in (t0, t0 + 1):
+                            mm8(accs[t, n], a, t, n, 0, N_TILE, a == 0)
+                    for n in range(2):
+                        for t in (t0, t0 + 1):
+                            mm4(accs[t, n], a, t, n, 0, N_TILE, False)
+                else:
+                    for t in (t0, t0 + 1):
+                        for n in range(2):
+                            mm8(accs[t, n], a, t, n, 0, N_TILE, False)
+                            mm4(accs[t, n], a, t, n, 0, N_TILE, True)
+                            drain(accs[t, n], t, n, 0, N_TILE)
+
+        for t in range(4):
+            if t < PASSES:
+                quantize(widen(t, 4, 2))
+            group(t, 2, 0, N_TILE)
+
+        for t in range(4, 8):
+            for n in range(3):
+                if t == 4:
+                    quantize(widen(n, 6, 2))
+                if t == 7 and n == 2:
+                    group(t, n, 0, 256)
+                    group(t, n, 256, 128)
+                    group(t, n, 384, 128)
+                else:
+                    group(t, n, 0, N_TILE)

@@ -72,11 +72,11 @@ def tile_mix_feat_tm_quad_none_kernel(tc, x, w4_words, w4_scales, w8_words, w8_s
         def widen(a, t0, nt):
             tile, c0 = raw[a, t0]
             width = nt * T_TILE
-            src = tile[:, :, c0 : c0 + width].rearrange("p j (c i) -> p c j i", i=4)
+            src = tile[:, :, c0 : c0 + width].rearrange("p j (c i) -> p c j i", i=2)
             lin = stage.tile([P, width * PACK], BF16, name="lin", align_bytes=256)
             sq = stage.tile([P, width * PACK], BF16, name="sq", align_bytes=256)
-            nc.vector.tensor_copy(out=lin[:].rearrange("p (c i j) -> p c j i", i=4, j=PACK), in_=src)
-            nc.scalar.activation(out=sq[:].rearrange("p (c i j) -> p c j i", i=4, j=PACK), in_=src, func=SQUARE)
+            nc.vector.tensor_copy(out=lin[:].rearrange("p (c i j) -> p c j i", i=2, j=PACK), in_=src)
+            nc.scalar.activation(out=sq[:].rearrange("p (c i j) -> p c j i", i=2, j=PACK), in_=src, func=SQUARE)
             return (a, t0, nt, lin, sq)
 
         def quantize(unit):
@@ -90,16 +90,16 @@ def tile_mix_feat_tm_quad_none_kernel(tc, x, w4_words, w4_scales, w8_words, w8_s
                     cols = slice((t - t0) * T_TILE, (t - t0 + 1) * T_TILE)
                     feats[kind, a, t] = (codes[:, cols], plane[:, cols])
 
-        def mm8(acc, a, t, n, c0, width, start):
+        def mm8(acc, a, t, n, c0, width, start, stop=False):
             codes, plane = feats["lin", a, t]
             nc.tensor.matmul_mx(
                 out=acc[:, 0:width],
                 lhsT=codes.bitcast(FP8X4),
                 lhsT_scale=plane,
                 rhs=w8[a, n][:, c0 : c0 + width].bitcast(FP8X4),
-                rhs_scale=plane8[W8_ROW:P, a, n * N_TILE + c0 : n * N_TILE + c0 + width],
+                rhs_scale=scale8[a, n][:, c0 : c0 + width],
                 start=start,
-                stop=False,
+                stop=stop,
             )
 
         def mm4(acc, a, t, n, c0, width, stop):
@@ -111,7 +111,7 @@ def tile_mix_feat_tm_quad_none_kernel(tc, x, w4_words, w4_scales, w8_words, w8_s
                     lhsT=codes.bitcast(FP8X4),
                     lhsT_scale=plane,
                     rhs=w4[a, n][:, 2 * (c0 + s) : 2 * (c0 + s + step)].bitcast(FP4X4),
-                    rhs_scale=plane4[:, a, n * N_TILE + c0 + s : n * N_TILE + c0 + s + step],
+                    rhs_scale=scale4[a, n][:, c0 + s : c0 + s + step],
                     start=False,
                     stop=stop and s + step == width,
                 )
@@ -135,26 +135,41 @@ def tile_mix_feat_tm_quad_none_kernel(tc, x, w4_words, w4_scales, w8_words, w8_s
                 mm4(acc, a, t, n, c0, width, a == PASSES - 1)
             drain(acc, t, n, c0, width)
 
-        plane8 = keep.tile([P, PASSES, M], U8, name="plane8", align_bytes=256)
-        plane4 = keep.tile([P, PASSES, M], U8, name="plane4", align_bytes=256)
+        plane8 = keep.tile([P, PASSES, 2 * N_TILE], U8, name="plane8", align_bytes=256)
+        plane4 = keep.tile([P, PASSES, 2 * N_TILE], U8, name="plane4", align_bytes=256)
+        plane_late = keep.tile([P, PASSES, N_TILE], U8, name="plane_late", align_bytes=256)
+        scale8 = {}
+        scale4 = {}
+        for a in range(PASSES):
+            for n in range(2):
+                scale8[a, n] = plane8[W8_ROW:P, a, n * N_TILE : (n + 1) * N_TILE]
+                scale4[a, n] = plane4[:, a, n * N_TILE : (n + 1) * N_TILE]
+            scale8[a, 2] = plane_late[W8_ROW:P, a, :]
+            scale4[a, 2] = plane_late[:, a, :]
         nc.vector.memset(plane8[:].bitcast(I32), 0)
         nc.vector.memset(plane4[:].bitcast(I32), 0)
+        nc.vector.memset(plane_late[:].bitcast(I32), 0)
 
         load_x(0, 0, 1)
         load_w8(0, 1, 0, 1)
-        load_scales(plane8, w8_scales, W8_ROW)
+        load_scales(plane8, w8_scales[:, :, 0 : 2 * N_TILE], W8_ROW)
         load_x(0, 1, 1)
         load_w8(0, 1, 1, 1)
+        load_x(0, 2, 1)
+        load_x(0, 3, 1)
         load_w4(0, 1, 0, 2)
-        load_x(0, 2, 2)
-        load_scales(plane4, w4_scales, 0)
+        load_scales(plane4, w4_scales[:, :, 0 : 2 * N_TILE], 0)
         for a in range(1, PASSES):
             load_x(a, 0, 2)
-            load_w8(a, 1, 0, 2)
             load_w4(a, 1, 0, 2)
-            load_x(a, 2, 2)
-        load_w8(0, PASSES, 2, 1)
-        load_w4(0, PASSES, 2, 1)
+            load_x(a, 2, 1)
+            load_w8(a, 1, 0, 2)
+            load_x(a, 3, 1)
+        load_scales(plane_late, w8_scales[:, :, 2 * N_TILE : M], W8_ROW)
+        load_scales(plane_late, w4_scales[:, :, 2 * N_TILE : M], 0)
+        for a in range(PASSES):
+            load_w8(a, 1, 2, 1)
+            load_w4(a, 1, 2, 1)
         for t0 in (4, 6):
             for a in range(PASSES):
                 load_x(a, t0, 2)
@@ -164,35 +179,42 @@ def tile_mix_feat_tm_quad_none_kernel(tc, x, w4_words, w4_scales, w8_words, w8_s
             for n in range(2):
                 acc = psum.tile([P, N_TILE], F32, name="acc")
                 accs[t, n] = acc
-        for a in range(PASSES):
-            for t0 in (0, 2):
-                if a == 0 and t0 == 0:
-                    quantize(widen(a, 0, 1))
-                    quantize(widen(a, 1, 1))
-                else:
-                    first = widen(a, t0, 1)
-                    second = widen(a, t0 + 1, 1)
-                    quantize(first)
-                    quantize(second)
-            for t0 in (0, 2):
-                if a < PASSES - 1:
+        for t in range(4):
+            quantize(widen(0, t, 1))
+        for t, n in ((0, 0), (1, 0), (0, 1), (1, 1), (2, 0), (2, 1), (3, 0), (3, 1)):
+            mm8(accs[t, n], 0, t, n, 0, N_TILE, True)
+        for t in range(4):
+            for n in range(2):
+                mm4(accs[t, n], 0, t, n, 0, N_TILE, False)
+        for a in range(1, PASSES):
+            last = a == PASSES - 1
+            first = widen(a, 0, 1)
+            second = widen(a, 1, 1)
+            quantize(first)
+            quantize(second)
+            quantize(widen(a, 2, 1))
+            quantize(widen(a, 3, 1))
+            for tiles in ((0, 1, 2), (3,)):
+                for t in tiles:
                     for n in range(2):
-                        for t in (t0, t0 + 1):
-                            mm8(accs[t, n], a, t, n, 0, N_TILE, a == 0)
+                        mm4(accs[t, n], a, t, n, 0, N_TILE, False)
+                for t in tiles:
                     for n in range(2):
-                        for t in (t0, t0 + 1):
-                            mm4(accs[t, n], a, t, n, 0, N_TILE, False)
-                else:
-                    for t in (t0, t0 + 1):
-                        for n in range(2):
-                            mm8(accs[t, n], a, t, n, 0, N_TILE, False)
-                            mm4(accs[t, n], a, t, n, 0, N_TILE, True)
+                        mm8(accs[t, n], a, t, n, 0, N_TILE, False, last)
+                        if last:
                             drain(accs[t, n], t, n, 0, N_TILE)
 
         for t in range(4):
-            if t < PASSES:
-                quantize(widen(t, 4, 2))
-            group(t, 2, 0, N_TILE)
+            acc = psum.tile([P, N_TILE], F32, name="acc")
+            accs[t, 2] = acc
+        for a in range(PASSES):
+            quantize(widen(a, 4, 2))
+            for t in range(4):
+                mm8(accs[t, 2], a, t, 2, 0, N_TILE, a == 0)
+            for t in range(4):
+                mm4(accs[t, 2], a, t, 2, 0, N_TILE, a == PASSES - 1)
+                if a == PASSES - 1:
+                    drain(accs[t, 2], t, 2, 0, N_TILE)
 
         for t in range(4, 8):
             for n in range(3):

@@ -29,7 +29,6 @@ def tile_mix_feat_tm_quad_none_kernel(tc, x, w4_words, w4_scales, w8_words, w8_s
     with ExitStack() as ctx:
         keep = ctx.enter_context(tc.tile_pool(name="keep", bufs=1))
         stage = ctx.enter_context(tc.tile_pool(name="stage", bufs=4))
-        results = ctx.enter_context(tc.tile_pool(name="results", bufs=16))
         psum = ctx.enter_context(tc.psum_pool(name="psum", bufs=8))
         ctx.enter_context(tc.manual_schedule())
 
@@ -90,7 +89,7 @@ def tile_mix_feat_tm_quad_none_kernel(tc, x, w4_words, w4_scales, w8_words, w8_s
                     cols = slice((t - t0) * T_TILE, (t - t0 + 1) * T_TILE)
                     feats[kind, a, t] = (codes[:, cols], plane[:, cols])
 
-        def mm8(acc, a, t, n, c0, width, start, stop=False):
+        def mm8(acc, a, t, n, c0, width, start, stop):
             codes, plane = feats["lin", a, t]
             nc.tensor.matmul_mx(
                 out=acc[:, 0:width],
@@ -102,7 +101,7 @@ def tile_mix_feat_tm_quad_none_kernel(tc, x, w4_words, w4_scales, w8_words, w8_s
                 stop=stop,
             )
 
-        def mm4(acc, a, t, n, c0, width, stop):
+        def mm4(acc, a, t, n, c0, width, start, stop):
             codes, plane = feats["sq", a, t]
             step = N_TILE if width == N_TILE else 128
             for s in range(0, width, step):
@@ -112,28 +111,45 @@ def tile_mix_feat_tm_quad_none_kernel(tc, x, w4_words, w4_scales, w8_words, w8_s
                     lhsT_scale=plane,
                     rhs=w4[a, n][:, 2 * (c0 + s) : 2 * (c0 + s + step)].bitcast(FP4X4),
                     rhs_scale=scale4[a, n][:, c0 + s : c0 + s + step],
-                    start=False,
+                    start=start and s == 0,
                     stop=stop and s + step == width,
                 )
 
         drained = []
+        rows_out = {}
+        for t in range(T // T_TILE):
+            rows_out[t] = keep.tile([P, M], F32, name="rows_out_%d" % t)
 
         def drain(acc, t, n, c0, width):
-            res = results.tile([P, width], F32, name="res")
-            if len(drained) % 2 == 0:
-                nc.scalar.copy(out=res[:], in_=acc[:, 0:width])
-            else:
-                nc.vector.tensor_copy(out=res[:], in_=acc[:, 0:width])
-            drained.append((t, n, c0))
             col = n * N_TILE + c0
-            nc.sync.dma_start(out=out[t * T_TILE : (t + 1) * T_TILE, col : col + width], in_=res[:])
+            if len(drained) % 2 == 0:
+                nc.scalar.copy(out=rows_out[t][:, col : col + width], in_=acc[:, 0:width])
+            else:
+                nc.vector.tensor_copy(out=rows_out[t][:, col : col + width], in_=acc[:, 0:width])
+            drained.append((t, n, c0))
 
-        def group(t, n, c0, width):
-            acc = psum.tile([P, N_TILE], F32, name="acc")
-            for a in range(PASSES):
-                mm8(acc, a, t, n, c0, width, a == 0)
-                mm4(acc, a, t, n, c0, width, a == PASSES - 1)
-            drain(acc, t, n, c0, width)
+        def store(t, col, width):
+            nc.sync.dma_start(out=out[t * T_TILE : (t + 1) * T_TILE, col : col + width], in_=rows_out[t][:, col : col + width])
+
+        accs = {}
+        done = {}
+
+        def run(mm, a, groups, c0=0, width=N_TILE):
+            for t, n in groups:
+                count = done.get((t, n, c0), 0)
+                if count == 0:
+                    acc = psum.tile([P, N_TILE], F32, name="acc")
+                    accs[t, n, c0] = acc
+                last = count == 2 * PASSES - 1
+                mm(accs[t, n, c0], a, t, n, c0, width, count == 0, last)
+                done[t, n, c0] = count + 1
+                if last:
+                    drain(accs[t, n, c0], t, n, c0, width)
+
+        def group(t, n, c0, width, order):
+            for mm in order:
+                for a in range(PASSES):
+                    run(mm, a, [(t, n)], c0, width)
 
         plane8 = keep.tile([P, PASSES, 2 * N_TILE], U8, name="plane8", align_bytes=256)
         plane4 = keep.tile([P, PASSES, 2 * N_TILE], U8, name="plane4", align_bytes=256)
@@ -167,62 +183,54 @@ def tile_mix_feat_tm_quad_none_kernel(tc, x, w4_words, w4_scales, w8_words, w8_s
             load_x(a, 3, 1)
         load_scales(plane_late, w8_scales[:, :, 2 * N_TILE : M], W8_ROW)
         load_scales(plane_late, w4_scales[:, :, 2 * N_TILE : M], 0)
+        load_w8(0, 1, 2, 1)
+        load_w4(0, PASSES, 2, 1)
+        load_w8(1, PASSES - 1, 2, 1)
         for a in range(PASSES):
-            load_w8(a, 1, 2, 1)
-            load_w4(a, 1, 2, 1)
-        for t0 in (4, 6):
-            for a in range(PASSES):
-                load_x(a, t0, 2)
+            load_x(a, 4, 4)
 
-        accs = {}
-        for t in range(4):
-            for n in range(2):
-                acc = psum.tile([P, N_TILE], F32, name="acc")
-                accs[t, n] = acc
         for t in range(4):
             quantize(widen(0, t, 1))
-        for t, n in ((0, 0), (1, 0), (0, 1), (1, 1), (2, 0), (2, 1), (3, 0), (3, 1)):
-            mm8(accs[t, n], 0, t, n, 0, N_TILE, True)
-        for t in range(4):
-            for n in range(2):
-                mm4(accs[t, n], 0, t, n, 0, N_TILE, False)
+        run(mm8, 0, [(0, 0), (1, 0), (0, 1), (1, 1), (2, 0), (2, 1), (3, 0), (3, 1)])
+        run(mm4, 0, [(t, n) for t in range(4) for n in range(2)])
         for a in range(1, PASSES):
-            last = a == PASSES - 1
             first = widen(a, 0, 1)
             second = widen(a, 1, 1)
             quantize(first)
             quantize(second)
             quantize(widen(a, 2, 1))
             quantize(widen(a, 3, 1))
-            for tiles in ((0, 1, 2), (3,)):
-                for t in tiles:
-                    for n in range(2):
-                        mm4(accs[t, n], a, t, n, 0, N_TILE, False)
-                for t in tiles:
-                    for n in range(2):
-                        mm8(accs[t, n], a, t, n, 0, N_TILE, False, last)
-                        if last:
-                            drain(accs[t, n], t, n, 0, N_TILE)
+            for tiles, order in (((0, 1, 2), (mm4, mm8)), ((3,), (mm8, mm4))):
+                for mm in order:
+                    run(mm, a, [(t, n) for t in tiles for n in range(2)])
 
-        for t in range(4):
-            acc = psum.tile([P, N_TILE], F32, name="acc")
-            accs[t, 2] = acc
+        quantize(widen(0, 4, 2))
+        last_column = [(t, 2) for t in range(4)]
+        run(mm8, 0, last_column)
         for a in range(PASSES):
-            quantize(widen(a, 4, 2))
-            for t in range(4):
-                mm8(accs[t, 2], a, t, 2, 0, N_TILE, a == 0)
-            for t in range(4):
-                mm4(accs[t, 2], a, t, 2, 0, N_TILE, a == PASSES - 1)
-                if a == PASSES - 1:
-                    drain(accs[t, 2], t, 2, 0, N_TILE)
+            run(mm4, a, last_column)
+        for a in range(1, PASSES):
+            run(mm8, a, last_column)
+        for t in range(4):
+            store(t, 0, M)
 
-        for t in range(4, 8):
-            for n in range(3):
-                if t == 4:
-                    quantize(widen(n, 6, 2))
-                if t == 7 and n == 2:
-                    group(t, n, 0, 256)
-                    group(t, n, 256, 128)
-                    group(t, n, 384, 128)
-                else:
-                    group(t, n, 0, N_TILE)
+        quantize(widen(0, 6, 2))
+        for a in range(1, PASSES):
+            quantize(widen(a, 4, 2))
+            quantize(widen(a, 6, 2))
+        pair = [(t, n) for t in (4, 5) for n in range(3)]
+        for a in range(PASSES):
+            for mm in ((mm8, mm4) if a % 2 == 0 else (mm4, mm8)):
+                run(mm, a, pair)
+        for t in (4, 5):
+            store(t, 0, M)
+
+        for n in range(3):
+            group(6, n, 0, N_TILE, (mm4, mm8) if n % 2 == 0 else (mm8, mm4))
+        store(6, 0, M)
+        for n in range(2):
+            group(7, n, 0, N_TILE, (mm8, mm4) if n % 2 == 0 else (mm4, mm8))
+            store(7, n * N_TILE, N_TILE)
+        for c0, width, order in ((0, 256, (mm8, mm4)), (256, 128, (mm4, mm8)), (384, 128, (mm8, mm4))):
+            group(7, 2, c0, width, order)
+            store(7, 2 * N_TILE + c0, width)

@@ -20,7 +20,20 @@ K_PASS = P * PACK
 PASSES = K // K_PASS
 T_TILE = 128
 N_TILE = 512
+T_TILES = T // T_TILE
+N_TILES = M // N_TILE
+BANKS = 8
+QUADRANT = 32
+SCALE_ROWS = 4
+ALIGN = 256
 W8_ROW = 4
+FIRST_T = 4
+FIRST_N = 2
+LAST_N = N_TILES - 1
+NEIGHBOURS = 2
+STAGE_BUFS = 4
+NARROW = 128
+LAST_PIECES = (256, 128, 128)
 
 
 def tile_mix_feat_tm_quad_none_kernel(tc, x, w4_words, w4_scales, w8_words, w8_scales, out):
@@ -28,97 +41,99 @@ def tile_mix_feat_tm_quad_none_kernel(tc, x, w4_words, w4_scales, w8_words, w8_s
 
     with ExitStack() as ctx:
         keep = ctx.enter_context(tc.tile_pool(name="keep", bufs=1))
-        stage = ctx.enter_context(tc.tile_pool(name="stage", bufs=4))
-        psum = ctx.enter_context(tc.psum_pool(name="psum", bufs=8))
+        stage = ctx.enter_context(tc.tile_pool(name="stage", bufs=STAGE_BUFS))
+        psum = ctx.enter_context(tc.psum_pool(name="psum", bufs=BANKS))
         ctx.enter_context(tc.manual_schedule())
 
         w8_bytes = w8_words.rearrange("a p n i -> p a (n i)")
         w4_bytes = w4_words.rearrange("a p b -> p a b")
 
-        raw = {}
-        w8 = {}
-        w4 = {}
-        feats = {}
+        x_raw = {}
+        w8_codes = {}
+        w4_codes = {}
+        w8_plane = {}
+        w4_plane = {}
+        quantised = {}
 
-        def load_x(a, t0, nt):
-            tile = keep.tile([P, PACK, nt * T_TILE], F32, name="x_%d_%d" % (a, t0))
-            rows = x[a * K_PASS : (a + 1) * K_PASS, t0 * T_TILE : (t0 + nt) * T_TILE]
+        def load_x(a, t0, tiles):
+            tile = keep.tile([P, PACK, tiles * T_TILE], F32, name="x_%d_%d" % (a, t0))
+            rows = x[a * K_PASS : (a + 1) * K_PASS, t0 * T_TILE : (t0 + tiles) * T_TILE]
             nc.sync.dma_start(out=tile[:], in_=rows.rearrange("(p j) w -> p j w", j=PACK))
-            for t in range(t0, t0 + nt):
-                raw[a, t] = (tile, (t - t0) * T_TILE)
+            for t in range(t0, t0 + tiles):
+                x_raw[a, t] = (tile, (t - t0) * T_TILE)
 
-        def load_w8(a0, na, n0, nn):
-            tile = keep.tile([P, na, nn * N_TILE], U32, name="w8_%d_%d" % (a0, n0), align_bytes=256)
-            src = w8_bytes[:, a0 : a0 + na, 4 * n0 * N_TILE : 4 * (n0 + nn) * N_TILE]
+        def load_w8(a0, passes, n0, tiles):
+            tile = keep.tile([P, passes, tiles * N_TILE], U32, name="w8_%d_%d" % (a0, n0), align_bytes=ALIGN)
+            src = w8_bytes[:, a0 : a0 + passes, 4 * n0 * N_TILE : 4 * (n0 + tiles) * N_TILE]
             nc.sync.dma_start(out=tile[:].bitcast(I32), in_=src.bitcast(I32))
-            for a in range(a0, a0 + na):
-                for n in range(n0, n0 + nn):
-                    w8[a, n] = tile[:, a - a0, (n - n0) * N_TILE : (n - n0 + 1) * N_TILE]
+            for a in range(a0, a0 + passes):
+                for n in range(n0, n0 + tiles):
+                    w8_codes[a, n] = tile[:, a - a0, (n - n0) * N_TILE : (n - n0 + 1) * N_TILE]
 
-        def load_w4(a0, na, n0, nn):
-            tile = keep.tile([P, na, 2 * nn * N_TILE], U8, name="w4_%d_%d" % (a0, n0), align_bytes=256)
-            src = w4_bytes[:, a0 : a0 + na, 2 * n0 * N_TILE : 2 * (n0 + nn) * N_TILE]
+        def load_w4(a0, passes, n0, tiles):
+            tile = keep.tile([P, passes, 2 * tiles * N_TILE], U8, name="w4_%d_%d" % (a0, n0), align_bytes=ALIGN)
+            src = w4_bytes[:, a0 : a0 + passes, 2 * n0 * N_TILE : 2 * (n0 + tiles) * N_TILE]
             nc.sync.dma_start(out=tile[:].bitcast(I32), in_=src.bitcast(I32))
-            for a in range(a0, a0 + na):
-                for n in range(n0, n0 + nn):
-                    w4[a, n] = tile[:, a - a0, 2 * (n - n0) * N_TILE : 2 * (n - n0 + 1) * N_TILE]
+            for a in range(a0, a0 + passes):
+                for n in range(n0, n0 + tiles):
+                    w4_codes[a, n] = tile[:, a - a0, 2 * (n - n0) * N_TILE : 2 * (n - n0 + 1) * N_TILE]
 
-        def load_scales(plane, scales, row0):
-            by_row = scales.rearrange("a (q r) n -> r q a n", r=4)
-            for r in range(4):
-                nc.sync.dma_start(out=plane[row0 + r : P : 32, :, :].bitcast(I32), in_=by_row[r].bitcast(I32))
+        def load_scales(queue, plane, scales, row0):
+            by_row = scales.rearrange("a (q r) n -> r q a n", r=SCALE_ROWS)
+            for r in range(SCALE_ROWS):
+                queue.dma_start(out=plane[row0 + r : P : QUADRANT, :, :].bitcast(I32), in_=by_row[r].bitcast(I32))
 
-        def widen(a, t0, nt):
-            tile, c0 = raw[a, t0]
-            width = nt * T_TILE
-            src = tile[:, :, c0 : c0 + width].rearrange("p j (c i) -> p c j i", i=2)
-            lin = stage.tile([P, width * PACK], BF16, name="lin", align_bytes=256)
-            sq = stage.tile([P, width * PACK], BF16, name="sq", align_bytes=256)
-            nc.vector.tensor_copy(out=lin[:].rearrange("p (c i j) -> p c j i", i=2, j=PACK), in_=src)
-            nc.scalar.activation(out=sq[:].rearrange("p (c i j) -> p c j i", i=2, j=PACK), in_=src, func=SQUARE)
-            return (a, t0, nt, lin, sq)
+        def interleave(a, t0, tiles):
+            tile, c0 = x_raw[a, t0]
+            width = tiles * T_TILE
+            src = tile[:, :, c0 : c0 + width].rearrange("p j (c i) -> p c j i", i=NEIGHBOURS)
+            xb = stage.tile([P, width * PACK], BF16, name="xb", align_bytes=ALIGN)
+            xa = stage.tile([P, width * PACK], BF16, name="xa", align_bytes=ALIGN)
+            nc.vector.tensor_copy(out=xb[:].rearrange("p (c i j) -> p c j i", i=NEIGHBOURS, j=PACK), in_=src)
+            nc.scalar.activation(out=xa[:].rearrange("p (c i j) -> p c j i", i=NEIGHBOURS, j=PACK), in_=src, func=SQUARE)
+            return (a, t0, tiles, xb, xa)
 
-        def quantize(unit):
-            a, t0, nt, lin, sq = unit
-            width = nt * T_TILE
-            for kind, src in (("lin", lin), ("sq", sq)):
-                codes = keep.tile([P, width], U32, name="%s_codes_%d_%d" % (kind, a, t0), align_bytes=256)
-                plane = keep.tile([P, width], U8, name="%s_plane_%d_%d" % (kind, a, t0), align_bytes=256)
-                nc.vector.quantize_mx(out=codes[:].bitcast(FP8X4), scales=plane[:], in_=src[:])
-                for t in range(t0, t0 + nt):
+        def quantize(staged):
+            a, t0, tiles, xb, xa = staged
+            width = tiles * T_TILE
+            for operand, values in (("xb", xb), ("xa", xa)):
+                codes = keep.tile([P, width], U32, name="%s_codes_%d_%d" % (operand, a, t0), align_bytes=ALIGN)
+                plane = keep.tile([P, width], U8, name="%s_plane_%d_%d" % (operand, a, t0), align_bytes=ALIGN)
+                nc.vector.quantize_mx(out=codes[:].bitcast(FP8X4), scales=plane[:], in_=values[:])
+                for t in range(t0, t0 + tiles):
                     cols = slice((t - t0) * T_TILE, (t - t0 + 1) * T_TILE)
-                    feats[kind, a, t] = (codes[:, cols], plane[:, cols])
+                    quantised[operand, a, t] = (codes[:, cols], plane[:, cols])
 
-        def mm8(acc, a, t, n, c0, width, start, stop):
-            codes, plane = feats["lin", a, t]
+        def linear(acc, a, t, n, c0, width, start, stop):
+            codes, plane = quantised["xb", a, t]
             nc.tensor.matmul_mx(
                 out=acc[:, 0:width],
                 lhsT=codes.bitcast(FP8X4),
                 lhsT_scale=plane,
-                rhs=w8[a, n][:, c0 : c0 + width].bitcast(FP8X4),
-                rhs_scale=scale8[a, n][:, c0 : c0 + width],
+                rhs=w8_codes[a, n][:, c0 : c0 + width].bitcast(FP8X4),
+                rhs_scale=w8_plane[a, n][:, c0 : c0 + width],
                 start=start,
                 stop=stop,
             )
 
-        def mm4(acc, a, t, n, c0, width, start, stop):
-            codes, plane = feats["sq", a, t]
-            step = N_TILE if width == N_TILE else 128
+        def square(acc, a, t, n, c0, width, start, stop):
+            codes, plane = quantised["xa", a, t]
+            step = N_TILE if width == N_TILE else NARROW
             for s in range(0, width, step):
                 nc.tensor.matmul_mx(
                     out=acc[:, s : s + step],
                     lhsT=codes.bitcast(FP8X4),
                     lhsT_scale=plane,
-                    rhs=w4[a, n][:, 2 * (c0 + s) : 2 * (c0 + s + step)].bitcast(FP4X4),
-                    rhs_scale=scale4[a, n][:, c0 + s : c0 + s + step],
+                    rhs=w4_codes[a, n][:, 2 * (c0 + s) : 2 * (c0 + s + step)].bitcast(FP4X4),
+                    rhs_scale=w4_plane[a, n][:, c0 + s : c0 + s + step],
                     start=start and s == 0,
                     stop=stop and s + step == width,
                 )
 
-        drained = []
         rows_out = {}
-        for t in range(T // T_TILE):
+        for t in range(T_TILES):
             rows_out[t] = keep.tile([P, M], F32, name="rows_out_%d" % t)
+        drained = []
 
         def drain(acc, t, n, c0, width):
             col = n * N_TILE + c0
@@ -131,106 +146,115 @@ def tile_mix_feat_tm_quad_none_kernel(tc, x, w4_words, w4_scales, w8_words, w8_s
         def store(t, col, width):
             nc.sync.dma_start(out=out[t * T_TILE : (t + 1) * T_TILE, col : col + width], in_=rows_out[t][:, col : col + width])
 
-        accs = {}
-        done = {}
+        banks = {}
+        passes_done = {}
 
-        def run(mm, a, groups, c0=0, width=N_TILE):
+        def run(product, a, groups, c0=0, width=N_TILE):
             for t, n in groups:
-                count = done.get((t, n, c0), 0)
+                count = passes_done.get((t, n, c0), 0)
                 if count == 0:
                     acc = psum.tile([P, N_TILE], F32, name="acc")
-                    accs[t, n, c0] = acc
+                    banks[t, n, c0] = acc
                 last = count == 2 * PASSES - 1
-                mm(accs[t, n, c0], a, t, n, c0, width, count == 0, last)
-                done[t, n, c0] = count + 1
+                product(banks[t, n, c0], a, t, n, c0, width, count == 0, last)
+                passes_done[t, n, c0] = count + 1
                 if last:
-                    drain(accs[t, n, c0], t, n, c0, width)
+                    drain(banks[t, n, c0], t, n, c0, width)
 
-        def group(t, n, c0, width, order):
-            for mm in order:
+        def whole_group(t, n, c0, width, products):
+            for product in products:
                 for a in range(PASSES):
-                    run(mm, a, [(t, n)], c0, width)
+                    run(product, a, [(t, n)], c0, width)
 
-        plane8 = keep.tile([P, PASSES, 2 * N_TILE], U8, name="plane8", align_bytes=256)
-        plane4 = keep.tile([P, PASSES, 2 * N_TILE], U8, name="plane4", align_bytes=256)
-        plane_late = keep.tile([P, PASSES, N_TILE], U8, name="plane_late", align_bytes=256)
-        scale8 = {}
-        scale4 = {}
-        for a in range(PASSES):
-            for n in range(2):
-                scale8[a, n] = plane8[W8_ROW:P, a, n * N_TILE : (n + 1) * N_TILE]
-                scale4[a, n] = plane4[:, a, n * N_TILE : (n + 1) * N_TILE]
-            scale8[a, 2] = plane_late[W8_ROW:P, a, :]
-            scale4[a, 2] = plane_late[:, a, :]
-        nc.vector.memset(plane8[:].bitcast(I32), 0)
-        nc.vector.memset(plane4[:].bitcast(I32), 0)
-        nc.vector.memset(plane_late[:].bitcast(I32), 0)
+        def turn(i):
+            return (linear, square) if i % 2 == 0 else (square, linear)
+
+        first_cols = FIRST_N * N_TILE
+        plane8_first = keep.tile([P, 1, M], U8, name="plane8_first", align_bytes=ALIGN)
+        plane8_rest = keep.tile([P, PASSES - 1, M], U8, name="plane8_rest", align_bytes=ALIGN)
+        plane4_first = keep.tile([P, PASSES, first_cols], U8, name="plane4_first", align_bytes=ALIGN)
+        plane4_last = keep.tile([P, PASSES, N_TILE], U8, name="plane4_last", align_bytes=ALIGN)
+        for n in range(N_TILES):
+            cols = slice(n * N_TILE, (n + 1) * N_TILE)
+            w8_plane[0, n] = plane8_first[W8_ROW:P, 0, cols]
+            for a in range(1, PASSES):
+                w8_plane[a, n] = plane8_rest[W8_ROW:P, a - 1, cols]
+            for a in range(PASSES):
+                w4_plane[a, n] = plane4_last[:, a, :] if n == LAST_N else plane4_first[:, a, cols]
+        for weight_plane in (plane8_first, plane8_rest, plane4_first):
+            nc.vector.memset(weight_plane[:].bitcast(I32), 0)
+
+        load_scales(nc.gpsimd, plane8_rest, w8_scales[1:PASSES], W8_ROW)
 
         load_x(0, 0, 1)
         load_w8(0, 1, 0, 1)
-        load_scales(plane8, w8_scales[:, :, 0 : 2 * N_TILE], W8_ROW)
+        load_scales(nc.sync, plane8_first, w8_scales[0:1], W8_ROW)
         load_x(0, 1, 1)
         load_w8(0, 1, 1, 1)
         load_x(0, 2, 1)
         load_x(0, 3, 1)
-        load_w4(0, 1, 0, 2)
-        load_scales(plane4, w4_scales[:, :, 0 : 2 * N_TILE], 0)
+        load_w4(0, 1, 0, FIRST_N)
+        load_scales(nc.sync, plane4_first, w4_scales[:, :, 0:first_cols], 0)
         for a in range(1, PASSES):
             load_x(a, 0, 2)
-            load_w4(a, 1, 0, 2)
+            load_w4(a, 1, 0, FIRST_N)
+            load_w8(a, 1, 0, FIRST_N)
             load_x(a, 2, 1)
-            load_w8(a, 1, 0, 2)
             load_x(a, 3, 1)
-        load_scales(plane_late, w8_scales[:, :, 2 * N_TILE : M], W8_ROW)
-        load_scales(plane_late, w4_scales[:, :, 2 * N_TILE : M], 0)
-        load_w8(0, 1, 2, 1)
-        load_w4(0, PASSES, 2, 1)
-        load_w8(1, PASSES - 1, 2, 1)
-        for a in range(PASSES):
-            load_x(a, 4, 4)
 
-        for t in range(4):
-            quantize(widen(0, t, 1))
-        run(mm8, 0, [(0, 0), (1, 0), (0, 1), (1, 1), (2, 0), (2, 1), (3, 0), (3, 1)])
-        run(mm4, 0, [(t, n) for t in range(4) for n in range(2)])
-        for a in range(1, PASSES):
-            first = widen(a, 0, 1)
-            second = widen(a, 1, 1)
-            quantize(first)
-            quantize(second)
-            quantize(widen(a, 2, 1))
-            quantize(widen(a, 3, 1))
-            for tiles, order in (((0, 1, 2), (mm4, mm8)), ((3,), (mm8, mm4))):
-                for mm in order:
-                    run(mm, a, [(t, n) for t in tiles for n in range(2)])
+        for t in range(FIRST_T):
+            quantize(interleave(0, t, 1))
 
-        quantize(widen(0, 4, 2))
-        last_column = [(t, 2) for t in range(4)]
-        run(mm8, 0, last_column)
+        nc.vector.memset(plane4_last[:].bitcast(I32), 0)
+        load_w8(0, 1, LAST_N, 1)
+        load_scales(nc.sync, plane4_last, w4_scales[:, :, first_cols:M], 0)
+        load_w4(0, PASSES, LAST_N, 1)
+        load_w8(1, PASSES - 1, LAST_N, 1)
         for a in range(PASSES):
-            run(mm4, a, last_column)
+            load_x(a, FIRST_T, T_TILES - FIRST_T)
+
+        run(linear, 0, [(t, n) for n in range(FIRST_N) for t in (0, 1)])
+        run(linear, 0, [(t, n) for t in (2, 3) for n in range(FIRST_N)])
+        run(square, 0, [(t, n) for t in range(FIRST_T) for n in range(FIRST_N)])
         for a in range(1, PASSES):
-            run(mm8, a, last_column)
-        for t in range(4):
+            staged = [interleave(a, t, 1) for t in (0, 1)]
+            for item in staged:
+                quantize(item)
+            for t in (2, 3):
+                quantize(interleave(a, t, 1))
+            for tiles, products in (((0, 1), (square, linear)), ((2,), (linear, square)), ((3,), (linear, square))):
+                for product in products:
+                    run(product, a, [(t, n) for t in tiles for n in range(FIRST_N)])
+
+        quantize(interleave(0, 4, 2))
+        last_column = [(t, LAST_N) for t in range(FIRST_T)]
+        run(linear, 0, last_column)
+        for a in range(PASSES):
+            run(square, a, last_column)
+        for a in range(1, PASSES):
+            run(linear, a, last_column)
+        for t in range(FIRST_T):
             store(t, 0, M)
 
-        quantize(widen(0, 6, 2))
         for a in range(1, PASSES):
-            quantize(widen(a, 4, 2))
-            quantize(widen(a, 6, 2))
-        pair = [(t, n) for t in (4, 5) for n in range(3)]
+            quantize(interleave(a, 4, 2))
+            quantize(interleave(a - 1, 6, 2))
+        quantize(interleave(PASSES - 1, 6, 2))
+        pair = [(t, n) for t in (4, 5) for n in range(N_TILES)]
         for a in range(PASSES):
-            for mm in ((mm8, mm4) if a % 2 == 0 else (mm4, mm8)):
-                run(mm, a, pair)
+            for product in turn(a):
+                run(product, a, pair)
         for t in (4, 5):
             store(t, 0, M)
 
-        for n in range(3):
-            group(6, n, 0, N_TILE, (mm4, mm8) if n % 2 == 0 else (mm8, mm4))
+        for n in range(N_TILES):
+            whole_group(6, n, 0, N_TILE, turn(n + 1))
         store(6, 0, M)
-        for n in range(2):
-            group(7, n, 0, N_TILE, (mm8, mm4) if n % 2 == 0 else (mm4, mm8))
+        for n in range(LAST_N):
+            whole_group(7, n, 0, N_TILE, turn(n))
             store(7, n * N_TILE, N_TILE)
-        for c0, width, order in ((0, 256, (mm8, mm4)), (256, 128, (mm4, mm8)), (384, 128, (mm8, mm4))):
-            group(7, 2, c0, width, order)
-            store(7, 2 * N_TILE + c0, width)
+        c0 = 0
+        for i, width in enumerate(LAST_PIECES):
+            whole_group(7, LAST_N, c0, width, turn(i))
+            store(7, LAST_N * N_TILE + c0, width)
+            c0 = c0 + width

from contextlib import ExitStack

import concourse.mybir as mybir

K, M, T = 1536, 1536, 1024
FLOPS = 2 * 2 * K * M * T

F32 = mybir.dt.float32
BF16 = mybir.dt.bfloat16
I32 = mybir.dt.int32
U32 = mybir.dt.uint32
U8 = mybir.dt.uint8
FP8X4 = mybir.dt.float8_e4m3fn_x4
FP4X4 = mybir.dt.float4_e2m1fn_x4
SQUARE = mybir.ActivationFunctionType.Square

P = 128
PACK = 4
K_PASS = P * PACK
PASSES = K // K_PASS
T_TILE = 128
N_TILE = 512
T_TILES = T // T_TILE
N_TILES = M // N_TILE
BANKS = 8
QUADRANT = 32
SCALE_ROWS = 4
ALIGN = 256
W8_ROW = 4
FIRST_T = 4
FIRST_N = 2
LAST_N = N_TILES - 1
NEIGHBOURS = 2
STAGE_BUFS = 4
NARROW = 128
LAST_PIECES = (256, 128, 128)


def tile_mix_feat_tm_quad_none_kernel(tc, x, w4_words, w4_scales, w8_words, w8_scales, out):
    nc = tc.nc

    with ExitStack() as ctx:
        keep = ctx.enter_context(tc.tile_pool(name="keep", bufs=1))
        stage = ctx.enter_context(tc.tile_pool(name="stage", bufs=STAGE_BUFS))
        psum = ctx.enter_context(tc.psum_pool(name="psum", bufs=BANKS))
        ctx.enter_context(tc.manual_schedule())

        w8_bytes = w8_words.rearrange("a p n i -> p a (n i)")
        w4_bytes = w4_words.rearrange("a p b -> p a b")

        x_raw = {}
        w8_codes = {}
        w4_codes = {}
        w8_plane = {}
        w4_plane = {}
        quantised = {}

        def load_x(a, t0, tiles):
            tile = keep.tile([P, PACK, tiles * T_TILE], F32, name="x_%d_%d" % (a, t0))
            rows = x[a * K_PASS : (a + 1) * K_PASS, t0 * T_TILE : (t0 + tiles) * T_TILE]
            nc.sync.dma_start(out=tile[:], in_=rows.rearrange("(p j) w -> p j w", j=PACK))
            for t in range(t0, t0 + tiles):
                x_raw[a, t] = (tile, (t - t0) * T_TILE)

        def load_w8(a0, passes, n0, tiles):
            tile = keep.tile([P, passes, tiles * N_TILE], U32, name="w8_%d_%d" % (a0, n0), align_bytes=ALIGN)
            src = w8_bytes[:, a0 : a0 + passes, 4 * n0 * N_TILE : 4 * (n0 + tiles) * N_TILE]
            nc.sync.dma_start(out=tile[:].bitcast(I32), in_=src.bitcast(I32))
            for a in range(a0, a0 + passes):
                for n in range(n0, n0 + tiles):
                    w8_codes[a, n] = tile[:, a - a0, (n - n0) * N_TILE : (n - n0 + 1) * N_TILE]

        def load_w4(a0, passes, n0, tiles):
            tile = keep.tile([P, passes, 2 * tiles * N_TILE], U8, name="w4_%d_%d" % (a0, n0), align_bytes=ALIGN)
            src = w4_bytes[:, a0 : a0 + passes, 2 * n0 * N_TILE : 2 * (n0 + tiles) * N_TILE]
            nc.sync.dma_start(out=tile[:].bitcast(I32), in_=src.bitcast(I32))
            for a in range(a0, a0 + passes):
                for n in range(n0, n0 + tiles):
                    w4_codes[a, n] = tile[:, a - a0, 2 * (n - n0) * N_TILE : 2 * (n - n0 + 1) * N_TILE]

        def load_scales(queue, plane, scales, row0):
            by_row = scales.rearrange("a (q r) n -> r q a n", r=SCALE_ROWS)
            for r in range(SCALE_ROWS):
                queue.dma_start(out=plane[row0 + r : P : QUADRANT, :, :].bitcast(I32), in_=by_row[r].bitcast(I32))

        def interleave(a, t0, tiles):
            tile, c0 = x_raw[a, t0]
            width = tiles * T_TILE
            src = tile[:, :, c0 : c0 + width].rearrange("p j (c i) -> p c j i", i=NEIGHBOURS)
            xb = stage.tile([P, width * PACK], BF16, name="xb", align_bytes=ALIGN)
            xa = stage.tile([P, width * PACK], BF16, name="xa", align_bytes=ALIGN)
            nc.vector.tensor_copy(out=xb[:].rearrange("p (c i j) -> p c j i", i=NEIGHBOURS, j=PACK), in_=src)
            nc.scalar.activation(out=xa[:].rearrange("p (c i j) -> p c j i", i=NEIGHBOURS, j=PACK), in_=src, func=SQUARE)
            return (a, t0, tiles, xb, xa)

        def quantize(staged):
            a, t0, tiles, xb, xa = staged
            width = tiles * T_TILE
            for operand, values in (("xb", xb), ("xa", xa)):
                codes = keep.tile([P, width], U32, name="%s_codes_%d_%d" % (operand, a, t0), align_bytes=ALIGN)
                plane = keep.tile([P, width], U8, name="%s_plane_%d_%d" % (operand, a, t0), align_bytes=ALIGN)
                nc.vector.quantize_mx(out=codes[:].bitcast(FP8X4), scales=plane[:], in_=values[:])
                for t in range(t0, t0 + tiles):
                    cols = slice((t - t0) * T_TILE, (t - t0 + 1) * T_TILE)
                    quantised[operand, a, t] = (codes[:, cols], plane[:, cols])

        def linear(acc, a, t, n, c0, width, start, stop):
            codes, plane = quantised["xb", a, t]
            nc.tensor.matmul_mx(
                out=acc[:, 0:width],
                lhsT=codes.bitcast(FP8X4),
                lhsT_scale=plane,
                rhs=w8_codes[a, n][:, c0 : c0 + width].bitcast(FP8X4),
                rhs_scale=w8_plane[a, n][:, c0 : c0 + width],
                start=start,
                stop=stop,
            )

        def square(acc, a, t, n, c0, width, start, stop):
            codes, plane = quantised["xa", a, t]
            step = N_TILE if width == N_TILE else NARROW
            for s in range(0, width, step):
                nc.tensor.matmul_mx(
                    out=acc[:, s : s + step],
                    lhsT=codes.bitcast(FP8X4),
                    lhsT_scale=plane,
                    rhs=w4_codes[a, n][:, 2 * (c0 + s) : 2 * (c0 + s + step)].bitcast(FP4X4),
                    rhs_scale=w4_plane[a, n][:, c0 + s : c0 + s + step],
                    start=start and s == 0,
                    stop=stop and s + step == width,
                )

        rows_out = {}
        for t in range(T_TILES):
            rows_out[t] = keep.tile([P, M], F32, name="rows_out_%d" % t)
        drained = []

        def drain(acc, t, n, c0, width):
            col = n * N_TILE + c0
            if len(drained) % 2 == 0:
                nc.scalar.copy(out=rows_out[t][:, col : col + width], in_=acc[:, 0:width])
            else:
                nc.vector.tensor_copy(out=rows_out[t][:, col : col + width], in_=acc[:, 0:width])
            drained.append((t, n, c0))

        def store(t, col, width):
            nc.sync.dma_start(out=out[t * T_TILE : (t + 1) * T_TILE, col : col + width], in_=rows_out[t][:, col : col + width])

        banks = {}
        passes_done = {}

        def run(product, a, groups, c0=0, width=N_TILE):
            for t, n in groups:
                count = passes_done.get((t, n, c0), 0)
                if count == 0:
                    acc = psum.tile([P, N_TILE], F32, name="acc")
                    banks[t, n, c0] = acc
                last = count == 2 * PASSES - 1
                product(banks[t, n, c0], a, t, n, c0, width, count == 0, last)
                passes_done[t, n, c0] = count + 1
                if last:
                    drain(banks[t, n, c0], t, n, c0, width)

        def whole_group(t, n, c0, width, products):
            for product in products:
                for a in range(PASSES):
                    run(product, a, [(t, n)], c0, width)

        def turn(i):
            return (linear, square) if i % 2 == 0 else (square, linear)

        first_cols = FIRST_N * N_TILE
        plane8_first = keep.tile([P, 1, M], U8, name="plane8_first", align_bytes=ALIGN)
        plane8_rest = keep.tile([P, PASSES - 1, M], U8, name="plane8_rest", align_bytes=ALIGN)
        plane4_first = keep.tile([P, PASSES, first_cols], U8, name="plane4_first", align_bytes=ALIGN)
        plane4_last = keep.tile([P, PASSES, N_TILE], U8, name="plane4_last", align_bytes=ALIGN)
        for n in range(N_TILES):
            cols = slice(n * N_TILE, (n + 1) * N_TILE)
            w8_plane[0, n] = plane8_first[W8_ROW:P, 0, cols]
            for a in range(1, PASSES):
                w8_plane[a, n] = plane8_rest[W8_ROW:P, a - 1, cols]
            for a in range(PASSES):
                w4_plane[a, n] = plane4_last[:, a, :] if n == LAST_N else plane4_first[:, a, cols]
        for weight_plane in (plane8_first, plane8_rest, plane4_first):
            nc.vector.memset(weight_plane[:].bitcast(I32), 0)

        load_scales(nc.gpsimd, plane8_rest, w8_scales[1:PASSES], W8_ROW)

        load_x(0, 0, 1)
        load_w8(0, 1, 0, 1)
        load_scales(nc.sync, plane8_first, w8_scales[0:1], W8_ROW)
        load_x(0, 1, 1)
        load_w8(0, 1, 1, 1)
        load_x(0, 2, 1)
        load_x(0, 3, 1)
        load_w4(0, 1, 0, FIRST_N)
        load_scales(nc.sync, plane4_first, w4_scales[:, :, 0:first_cols], 0)
        for a in range(1, PASSES):
            load_x(a, 0, 2)
            load_w4(a, 1, 0, FIRST_N)
            load_w8(a, 1, 0, FIRST_N)
            load_x(a, 2, 1)
            load_x(a, 3, 1)

        for t in range(FIRST_T):
            quantize(interleave(0, t, 1))

        nc.vector.memset(plane4_last[:].bitcast(I32), 0)
        load_w8(0, 1, LAST_N, 1)
        load_scales(nc.sync, plane4_last, w4_scales[:, :, first_cols:M], 0)
        load_w4(0, PASSES, LAST_N, 1)
        load_w8(1, PASSES - 1, LAST_N, 1)
        for a in range(PASSES):
            load_x(a, FIRST_T, T_TILES - FIRST_T)

        run(linear, 0, [(t, n) for n in range(FIRST_N) for t in (0, 1)])
        run(linear, 0, [(t, n) for t in (2, 3) for n in range(FIRST_N)])
        run(square, 0, [(t, n) for t in range(FIRST_T) for n in range(FIRST_N)])
        for a in range(1, PASSES):
            staged = [interleave(a, t, 1) for t in (0, 1)]
            for item in staged:
                quantize(item)
            for t in (2, 3):
                quantize(interleave(a, t, 1))
            for tiles, products in (((0, 1), (square, linear)), ((2,), (linear, square)), ((3,), (linear, square))):
                for product in products:
                    run(product, a, [(t, n) for t in tiles for n in range(FIRST_N)])

        quantize(interleave(0, 4, 2))
        last_column = [(t, LAST_N) for t in range(FIRST_T)]
        run(linear, 0, last_column)
        for a in range(PASSES):
            run(square, a, last_column)
        for a in range(1, PASSES):
            run(linear, a, last_column)
        for t in range(FIRST_T):
            store(t, 0, M)

        for a in range(1, PASSES):
            quantize(interleave(a, 4, 2))
            quantize(interleave(a - 1, 6, 2))
        quantize(interleave(PASSES - 1, 6, 2))
        pair = [(t, n) for t in (4, 5) for n in range(N_TILES)]
        for a in range(PASSES):
            for product in turn(a):
                run(product, a, pair)
        for t in (4, 5):
            store(t, 0, M)

        for n in range(N_TILES):
            whole_group(6, n, 0, N_TILE, turn(n + 1))
        store(6, 0, M)
        for n in range(LAST_N):
            whole_group(7, n, 0, N_TILE, turn(n))
            store(7, n * N_TILE, N_TILE)
        c0 = 0
        for i, width in enumerate(LAST_PIECES):
            whole_group(7, LAST_N, c0, width, turn(i))
            store(7, LAST_N * N_TILE + c0, width)
            c0 = c0 + width
